import numpy as np
CORES = [24,26,29,31,48,50,53,55]
N = 8
R, E = 4096, 2048
CAPP = 512
def entries(a): return a.T.reshape(-1)
def pack(v, P): return np.ascontiguousarray(np.asarray(v, np.int32).reshape(-1, P).T)
def lists(rng, how):
    n = N * E; q = np.arange(n) // E
    P = rng.permutation(np.repeat(np.arange(N * N), CAPP))[:n]
    if how == "full":
        a = rng.integers(0, N); z = np.delete(np.arange(N), a); o = rng.permutation(N * N); o = o[(o // N != a) & (o % N != a) & (o // N != o % N)]
        C = np.concatenate([N * a + rng.permutation(z), [(N + 1) * a], N * rng.permutation(z) + a, o])[:n // CAPP]
        L = np.repeat(C, CAPP).reshape(N, E); s, t = 1 + 2 * rng.integers(0, CAPP // 8, 2); t += 2 * (CAPP // 8)
        L[0, :s], L[1, :s] = C[E // CAPP], C[0]; L[0, s:s + t], L[N - 1, E - t:] = C[-1], C[0]
        L = L[rng.permutation(N)]; L[0] = L[0].reshape(16, -1).T.reshape(-1)
        for r in range(1, N, 2): L[r] = rng.permutation(L[r])
        P = L.reshape(-1)
    if how == "same":
        o = np.arange(N * N); o = rng.permutation(np.repeat(o[o % (N + 1) != 0], CAPP))[:n - N * CAPP].reshape(N, E - CAPP)
        P = np.stack([rng.permutation(np.append(o[r], np.full(CAPP, (N + 1) * r))) for r in range(N)]).reshape(-1)
    if how == "cross":
        d = np.stack([rng.permutation(1 + np.arange(E) % (N - 1)) for r in range(N)]).reshape(-1); a = 1 + rng.integers(0, N - 2, N); a += a >= N - np.arange(N)
        P = (q + a[d]) % N * N + (q + a[d] + d) % N
    if how == "edge": k = rng.permutation(n); P = k % (N * N)
    h, g = P // N, P % N; u, v = rng.integers(0, R, n), rng.integers(0, R, n)
    if how == "alike": u, v = rng.integers(0, R, N * N)[P], rng.integers(0, R, N * N)[P]
    if how == "edge": u, v = (R - 1) * (k // (N * N) % 2), (R - 1) * (k // (2 * N * N) % 2)
    if how == "full": u, v = (np.stack([rng.permutation(R)[np.arange(E) % R] for r in range(N)]).reshape(-1) for _ in range(2))
    if how == "same": v = u
    return {"pi": np.stack([pack(w, 16) for w in (R * h + u).reshape(N, E)]), "pj": np.stack([pack(w, 16) for w in (R * g + v).reshape(N, E)])}
def setup_inputs(rng):
    return dict({"ta": rng.standard_normal((N, 128, R), dtype=np.float32), "tb": rng.standard_normal((N, 128, R), dtype=np.float32)}, **lists(rng, "uniform"))
def setup_inputs_alike(rng):
    d = setup_inputs(rng); d.update(lists(rng, "alike"))
    for k in ("ta", "tb"): d[k] = (d[k].astype(np.float32) * 1024.0).astype(d[k].dtype)
    return d
def setup_inputs_cross(rng):
    d = setup_inputs(rng); d.update(lists(rng, "cross"))
    for k in ("ta", "tb"): d[k] = (d[k].astype(np.float32) * (1 / 1024.0)).astype(d[k].dtype)
    return d
def setup_inputs_edge(rng):
    d = setup_inputs(rng); d.update(lists(rng, "edge"))
    return d
def setup_inputs_full(rng):
    d = setup_inputs(rng); d.update(lists(rng, "full"))
    return d
def setup_inputs_same(rng):
    d = setup_inputs(rng); d.update(lists(rng, "same"))
    return d
def check_inputs(x):
    bad = []
    if x["pi"].min() < 0 or x["pi"].max() >= N * R: bad.append("pi out of range")
    if x["pj"].min() < 0 or x["pj"].max() >= N * R: bad.append("pj out of range")
    if not bad and int(np.bincount((x["pi"] // R * N + x["pj"] // R).reshape(-1), minlength=N * N).max()) > CAPP: bad.append("more than CAPP pairs with i in one rank's part of TA and j in one rank's part of TB")
    return bad
def reference(ta, tb, pi, pj):
    A, B = np.concatenate(list(ta), axis=1).astype(np.float64), np.concatenate(list(tb), axis=1).astype(np.float64)
    y = []
    for r in range(N):
        i, j = entries(pi[r]), entries(pj[r])
        y.append((A[:, i] * B[:, j]).sum(axis=0))
    return {"y": np.stack(y).reshape(N, -1, 16).transpose(0, 2, 1).astype(np.float32)}

@@ -1,0 +1,464 @@
+from concourse.bass import DstId, RemoteDMATransfer
+from concourse.mybir import dt, AluOpType, AxisListType, ActivationFunctionType
+
+NR = 8
+CAP = 512
+TRASH = 2048
+NK = 15
+SIM = 64
+A = AluOpType
+COPY = ActivationFunctionType.Copy
+
+SCRATCH = {
+    "ta_s": ("sbuf", [128, 4096], "float32"), "tb_s": ("sbuf", [128, 4096], "float32"),
+    "sb": ("sbuf", [128, 7 * CAP], "float32"), "rc": ("sbuf", [128, NR * CAP], "float32"),
+    "pr": ("sbuf", [128, 4 * CAP], "float32"),
+    "ni": ("sbuf", [128, 16], "int32"), "nj": ("sbuf", [128, 16], "int32"), "wr": ("sbuf", [128, 64], "int32"),
+    "t1": ("sbuf", [128, 16], "int32"), "t2": ("sbuf", [128, 16], "int32"),
+    "wa": ("sbuf", [128, 64], "int32"), "wb": ("sbuf", [128, 64], "int32"),
+    "wc": ("sbuf", [128, 64], "bfloat16"), "wd": ("sbuf", [128, 64], "bfloat16"),
+    "cl": ("sbuf", [128, 128], "bfloat16"), "w": ("sbuf", [128, 128, 4], "bfloat16"),
+    "d": ("sbuf", [128, 2048], "bfloat16"), "win": ("sbuf", [128, TRASH + NK * CAP], "bfloat16"),
+    "m": ("sbuf", [128, NK * 128], "bfloat16"), "s": ("sbuf", [128, NK * 128], "bfloat16"),
+    "z": ("sbuf", [128, NK * 128], "bfloat16"), "rst": ("sbuf", [128, 512], "bfloat16"),
+    "posf": ("sbuf", [128, 128], "float32"), "pos": ("sbuf", [128, 128], "uint16"), "gpos": ("sbuf", [128, 128], "uint16"),
+    "ev": ("sbuf", [128, NK * 16], "bfloat16"), "offv": ("sbuf", [128, 256], "uint16"), "offu": ("sbuf", [128, 256], "uint16"),
+    "pcol": ("sbuf", [128, 1], "int32"), "pb": ("sbuf", [128, 4], "int32"), "pf": ("sbuf", [128, 4], "float32"),
+    "mh": ("sbuf", [128, 1], "float32"), "q4": ("sbuf", [128, 4], "float32"), "my": ("sbuf", [128, 4], "float32"),
+    "wt": ("sbuf", [128, 4], "bfloat16"), "di": ("sbuf", [128, 128], "float32"), "jl": ("sbuf", [128, 128], "float32"),
+    "t16": ("sbuf", [128, 128], "float32"), "tr": ("sbuf", [128, 128], "float32"),
+    "ident": ("sbuf", [128, 128], "bfloat16"), "nu": ("sbuf", [128, 128], "bfloat16"), "one": ("sbuf", [128, 128], "bfloat16"),
+    "onef": ("sbuf", [128, 128], "float32"), "bi": ("sbuf", [128, NK * 128], "bfloat16"), "lk": ("sbuf", [128, 8 * 128], "bfloat16"),
+    "m16": ("sbuf", [128, 1024], "bfloat16"), "ry": ("sbuf", [128, 1024], "bfloat16"),
+    "scw": ("sbuf", [128, 4100], "float32"), "fin": ("sbuf", [128, 2048], "float32"), "fsc": ("sbuf", [128, 2048], "float32"),
+    "yp": ("sbuf", [128, 128], "float32"), "yl": ("sbuf", [128, 128], "float32"), "yh": ("sbuf", [128, 64], "float32"),
+    "y1": ("sbuf", [128, 64], "float32"), "y2": ("sbuf", [128, 32], "float32"), "y3": ("sbuf", [128, 16], "float32"),
+}
+for _i in range(8):
+    SCRATCH["ps%d" % _i] = ("psum", [128, 512], "float32")
+SEMAPHORES = ["sv", "ss", "sp", "sg", "dn", "dw", "lda", "ldb", "dy", "ls0", "ls", "cla", "wla", "ya", "hy"] + ["tb%d" % _i for _i in range(NR)]
+
+
+def bits(mask):
+    return [1 << e for e in range(32) if mask >> e & 1]
+
+
+def split(mask, n):
+    b = bits(mask)
+    k = 1
+    while 2 * k * n <= len(b):
+        k *= 2
+    return [sum(b[i * k:(i + 1) * k]) for i in range(n)]
+
+
+def count(mask):
+    return len(bits(mask))
+
+
+def plan(cores, topo):
+    P = {}
+    for c in cores:
+        on = [x for x in cores if topo.chip(x) == topo.chip(c)]
+        off = [x for x in cores if topo.chip(x) != topo.chip(c)]
+        s = on.index(c)
+        off = [off[(s + k) % len(off)] for k in range(len(off))]
+        near = [on[(s + k) % len(on)] for k in range(1, len(on))]
+        port = all(topo.may_write(c, d) for d in off)
+        far = topo.chip(off[0])
+        small, bulk = None, []
+        if not port:
+            free = [x for x in range(SIM) if x not in cores and topo.die(x) == topo.die(c) and all(topo.may_write(x, d) for d in off) and topo.may_write(c, x)]
+            small = [x for x in free if topo.chip(x) == topo.chip(c)][0]
+            bulk = [x for x in free if topo.mates(topo.chip(x), far) and topo.same_plane(topo.chip(x), topo.chip(c))]
+        mon, moff = topo.mask(c, near[0]), topo.mask(c, off[0])
+        P[c] = {"near": near, "off": off, "port": port, "small": small, "bulk": bulk, "mon": mon, "moff": moff, "min": mon & ~moff}
+    return P
+
+
+def rank_program(g, core, T, topo):
+    cores = list(T.cores)
+    P = plan(cores, topo)
+    rank = T.rank_of(core)
+    rk = {c: i for i, c in enumerate(cores)}
+
+    def dst(c):
+        a = topo.addr(c)
+        return DstId(rid=a[0], pnc=a[1])
+
+    def xfer(src, dsts, ids, mask, sem):
+        return RemoteDMATransfer(dst_ids=[dst(c) for c in ids], dma_engine_mask=mask, remote_sem=sem, srcs=[src], dsts=dsts)
+
+    ls = {"ls0": 0, "ls": 0}
+
+    def fused(xs, lsem="ls"):
+        g.remote_dma_fused([xfer(s, [d] * len(ids), ids, m, sem) for s, d, ids, m, sem in xs], local_sem=T.sem[lsem])
+        ls[lsem] += sum(count(x[3]) for x in xs)
+
+    def clc(r):
+        return T.cl[:, 16 * r:16 * r + 16]
+
+    def wc(r):
+        return T.w[:, 16 * r:16 * r + 16, :]
+
+    def rcc(r):
+        return T.rc[:, CAP * r:CAP * r + CAP]
+
+    def ylc(r):
+        return T.yl[:, 16 * r:16 * r + 16]
+
+    if rank is None:
+        for c in cores:
+            p = P[c]
+            r = rk[c]
+            if p["port"]:
+                continue
+            if core == p["small"]:
+                mo = topo.mask(core, p["off"][0])
+                g.wait_ge(T.sem.cla, count(p["mon"]))
+                fused([(clc(r), clc(r), p["off"], mo, T.sem.cla)])
+                g.wait_ge(T.sem.hy, count(p["mon"]))
+                b0 = min(rk[d] for d in p["off"])
+                ms = split(mo, len(p["off"]))
+                fused([(T.yh[:, 16 * (rk[d] - b0):16 * (rk[d] - b0) + 16], ylc(r), [d], ms[i], T.sem.ya) for i, d in enumerate(p["off"])])
+                g.wait_ge(T.sem.ls, ls["ls"])
+            if core in p["bulk"]:
+                nb = len(p["bulk"])
+                mine = p["off"][p["bulk"].index(core)::nb]
+                mo = topo.mask(core, mine[0])
+                g.wait_ge(T.sem.wla, count(p["moff"]))
+                fused([(wc(r), wc(r), mine, mo, T.sem.wla)])
+                for d in mine:
+                    q = rk[d]
+                    g.wait_ge(T.sem["tb%d" % q], count(p["moff"]))
+                    fused([(rcc(q), rcc(r), [d], mo, T.sem["tb%d" % r])])
+                g.wait_ge(T.sem.ls, ls["ls"])
+        return
+
+    a = rank
+    me = P[core]
+    near, off, port = me["near"], me["off"], me["port"]
+
+    eng = {"v": g.vector, "s": g.scalar, "p": g.tensor, "g": g, "y": g.sync}
+    psem = {"v": "sv", "s": "ss", "p": "sp", "g": "sg"}
+    done = {"v": 0, "s": 0, "p": 0, "g": 0}
+    seen = {}
+
+    def need(q, *toks):
+        for t in toks:
+            if t is None:
+                continue
+            if isinstance(t, list):
+                need(q, *t)
+                continue
+            sem, val = t
+            if seen.get((q, sem), 0) < val:
+                eng[q].wait_ge(T.sem[sem], val)
+                seen[(q, sem)] = val
+
+    def did(q, ins):
+        done[q] += 1
+        ins.then_inc(T.sem[psem[q]], 1)
+        return (psem[q], done[q])
+
+    V, S, PE = g.vector, g.scalar, g.tensor
+
+    def ts(out, in0, s1, s2, *ops):
+        return did("v", V.tensor_scalar(out, in0, s1, s2, *ops))
+
+    def tt(out, x, y, op):
+        return did("v", V.tensor_tensor(out, x, y, op))
+
+    def vcopy(out, x):
+        return did("v", V.tensor_copy(out, x))
+
+    def act(out, x, **kw):
+        return did("s", S.activation(out, x, COPY, **kw))
+
+    def mm(out, l, r, st, sp):
+        return did("p", PE.matmul(out, l, r, st, sp))
+
+    g.sync.dma_start(T.ni[:], T.pi[:]).then_inc(T.sem.dn, 16)
+    S.dma_start(T.nj[:], T.pj[:]).then_inc(T.sem.dn, 16)
+    g.sync.dma_start(T.wr[0::4, :], T.pi[:]).then_inc(T.sem.dw, 16)
+    g.sync.dma_start(T.wr[1::4, :], T.pi[:]).then_inc(T.sem.dw, 16)
+    S.dma_start(T.wr[2::4, :], T.pj[:]).then_inc(T.sem.dw, 16)
+    S.dma_start(T.wr[3::4, :], T.pj[:]).then_inc(T.sem.dw, 16)
+
+    F = dict(allow_small_or_imprecise_dtypes=True)
+    k_pcol = did("g", g.iota(T.pcol[:], [[0, 1]], 0, 1))
+    k_di = did("g", g.iota(T.di[:], [[1, 128]], 0, -1, **F))
+    k_q4 = did("g", g.iota(T.q4[:], [[1, 4]], 0, 0, **F))
+    k_t16 = did("g", g.iota(T.t16[:], [[16, 128]], 0, 0, **F))
+    k_jl = did("g", g.iota(T.jl[:], [[0, 8], [1, 16]], 0, 0, **F))
+
+    v_one = did("v", V.memset(T.one[:], 1.0))
+    did("v", V.memset(T.onef[:], 1.0))
+    v_r0 = did("v", V.memset(T.rst[:], 512.0))
+    need("v", k_pcol)
+    ts(T.pb[:, 0:1], T.pcol[:], 1, None, A.bitwise_and)
+    ts(T.pb[:, 1:2], T.pcol[:], 3, None, A.bitwise_and)
+    ts(T.pb[:, 2:3], T.pcol[:], 2, 3, A.arith_shift_right, A.bitwise_and)
+    v_pb = ts(T.pb[:, 3:4], T.pcol[:], 15, None, A.bitwise_and)
+    need("v", v_r0)
+    v_rst = did("v", V.memset(T.rst[:, 0::128], -2.0))
+    need("v", v_pb)
+    v_pf = vcopy(T.pf[:], T.pb[:])
+    need("v", k_di)
+    v_id = ts(T.ident[:], T.di[:], 0.0, None, A.is_equal)
+    v_nu = ts(T.nu[:], T.di[:], 0.0, -1.0, A.is_le, A.mult)
+    need("v", v_pf, k_q4, k_t16)
+    v_mh = ts(T.mh[:], T.pf[:, 0:1], 0.0, None, A.is_equal)
+    v_wt = ts(T.wt[:], T.q4[:], T.pf[:, 1:2], None, A.is_equal)
+    v_my = ts(T.my[:], T.q4[:], T.pf[:, 2:3], None, A.is_equal)
+    v_tr = ts(T.tr[:], T.t16[:], T.pf[:, 3:4], None, A.add)
+
+    need("v", ("dn", 32))
+    ts(T.t1[:], T.ni[:], 9, 56, A.arith_shift_right, A.bitwise_and)
+    x = ts(T.t2[:], T.nj[:], 12, None, A.arith_shift_right)
+    need("v", x)
+    v_cl = tt(clc(a), T.t1[:], T.t2[:], A.add)
+    need("v", ("dw", 64))
+    ts(T.wa[:], T.wr[:], 4032, None, A.bitwise_and)
+    x = ts(T.wb[:], T.wr[:], 63, None, A.bitwise_and)
+    need("v", x, v_mh)
+    ts(T.wc[:], T.wa[:], T.mh[:, 0:1], None, A.mult)
+    x = ts(T.wd[:], T.wb[:], T.pf[:, 0:1], None, A.mult)
+    need("v", x)
+    for b in range(4):
+        v_w = tt(T.w[:, 16 * a:16 * a + 16, b], T.wc[:, 16 * b:16 * b + 16], T.wd[:, 16 * b:16 * b + 16], A.add)
+    v_win = did("v", V.memset(T.win[:, TRASH:], 0.0))
+
+    need("g", v_cl)
+    if port:
+        fused([(clc(a), clc(a), near, me["min"], T.sem.cla), (clc(a), clc(a), off, me["moff"], T.sem.cla)], "ls0")
+    else:
+        fused([(clc(a), clc(a), near + [me["small"]], me["mon"], T.sem.cla)], "ls0")
+    need("g", v_w)
+    fused([(wc(a), wc(a), near, me["min"], T.sem.wla), (wc(a), wc(a), off if port else me["bulk"], me["moff"], T.sem.wla)], "ls0")
+    n_cl, n_w = 0, 0
+    for c in cores:
+        p = P[c]
+        if c == core:
+            continue
+        if c in near:
+            n_cl += count(p["min"] if p["port"] else p["mon"])
+            n_w += count(p["min"])
+        else:
+            n_cl += count(p["moff"] if p["port"] else topo.mask(p["small"], core))
+            n_w += count(p["moff"] if p["port"] else topo.mask(p["bulk"][0], core))
+
+    g.sync.wait_ge(T.sem.ls0, ls["ls0"])
+    g.sync.dma_start(T.tb_s[:], T.tb[:]).then_inc(T.sem.ldb, 16)
+    g.sync.dma_start(T.ta_s[:], T.ta[:]).then_inc(T.sem.lda, 16)
+
+    need("g", v_one)
+    for k in range(8):
+        g_lk = did("g", g.affine_select(T.lk[:, 128 * k:128 * k + 128], T.one[:], [[0, 8], [-1, 16]], A.is_equal, 0.0, -16 * k, 1))
+    need("s", v_id)
+    for k in range(NK):
+        s_bi = act(T.bi[:, 128 * k:128 * k + 128], T.ident[:], scale=float(TRASH + CAP * k + CAP // 2))
+
+    def eta(c):
+        if c in near:
+            return 2.0 + P[c]["near"].index(core)
+        return P[c]["off"].index(core) + (0.0 if P[c]["port"] else 1.2)
+    srcs = sorted([c for c in cores if c != core], key=eta)
+    cls = [8 * rk[d] + a for d in off + near] + [9 * a] + [8 * a + rk[c] for c in srcs]
+    banks = [range(0, 4), range(4, 8), range(8, 12), range(12, NK)]
+    ps = [T["ps%d" % i] for i in range(8)]
+    need("v", ("cla", n_cl), v_cl)
+    tm, tsn = {}, {}
+
+    def span(b):
+        return slice(128 * banks[b][0], 128 * banks[b][-1] + 128)
+
+    def masks(b):
+        for k in banks[b]:
+            tm[b] = ts(T.m[:, 128 * k:128 * k + 128], T.cl[:], float(cls[k]), None, A.is_equal)
+
+    def scan(b):
+        need("v", tm[b], v_rst)
+        n = 128 * len(banks[b])
+        tsn[b] = did("v", V.tensor_tensor_scan(T.s[:, span(b)], T.rst[:, 0:n], T.m[:, span(b)], -2.0, A.min, A.add))
+    masks(0); masks(1); scan(0); masks(2); scan(1); masks(3); scan(2); scan(3)
+    first = [True]
+
+    def p_nu(b):
+        need("p", tm[b], v_nu, v_one)
+        mm(ps[b][:, 0:128 * len(banks[b])], T.nu[:], T.m[:, span(b)], True, False)
+
+    def p_base(b):
+        need("p", tm[b], s_bi)
+        for k in banks[b]:
+            mm(ps[4][:, 0:128], T.bi[:, 128 * k:128 * k + 128], T.m[:, 128 * k:128 * k + 128], first[0], False)
+            first[0] = False
+    trank = {}
+
+    def p_s(b):
+        need("p", tsn[b])
+        trank[b] = mm(ps[b][:, 0:128 * len(banks[b])], T.one[:], T.s[:, span(b)], False, True)
+    p_nu(0); p_base(0); p_nu(1); p_s(0); p_base(1); p_nu(2); p_s(1); p_base(2); p_nu(3); p_s(2); p_s(3); p_base(3)
+    for b in range(4):
+        need("v", trank[b])
+        x = tt(T.z[:, span(b)], ps[b][:, 0:128 * len(banks[b])], T.m[:, span(b)], A.mult)
+        need("p", x, v_id)
+        for k in banks[b]:
+            p_pos = mm(ps[4][:, 0:128], T.ident[:], T.z[:, 128 * k:128 * k + 128], False, k == NK - 1)
+    need("v", p_pos, v_tr)
+    v_posf = tt(T.posf[:], ps[4][:, 0:128], T.tr[:], A.max)
+    need("v", v_posf)
+    v_pos = vcopy(T.pos[:], T.posf[:])
+
+    need("s", ("wla", n_w), v_w, v_my)
+    for yy in range(4):
+        for b in range(4):
+            s_d = act(T.d[:, 4 * yy + b::16], T.w[:, :, b], scale=T.my[:, yy:yy + 1])
+
+    need("v", v_pos, s_d, v_win)
+    v_sc = vcopy(T.win[:, :].indirect(T.pos[:, 0:128]), T.d[:])
+    v_gp = ts(T.gpos[:], T.posf[:], float(-(TRASH + 7 * CAP) + 1), 0.0, A.add, A.max)
+
+    def blocks(ks, bank):
+        need("p", v_sc, v_wt)
+        for k in ks:
+            for j in range(4):
+                c0 = TRASH + CAP * k + 128 * j
+                o = 4 * (4 * (k - ks[0]) + j)
+                t = mm(ps[bank][:, o:o + 4], T.win[:, c0:c0 + 128], T.wt[:], True, True)
+        return t
+
+    def evac(ks, bank, tok):
+        need("v", tok)
+        return vcopy(T.ev[:, 16 * ks[0]:16 * ks[-1] + 16], ps[bank][:, 0:16 * len(ks)])
+
+    def lists(ks, qt, bank, o, tok):
+        need("p", tok, g_lk)
+        n = 4 * len(ks)
+        for k in range(8):
+            for q in range(2):
+                t = mm(ps[bank][:, o + k:o + 8 * n:8], T.lk[:, 128 * k:128 * k + 128], T.ev[:, 16 * ks[0] + qt + q:16 * ks[-1] + 16:4], q == 0, q == 1)
+        return t
+    ka, kb, kc = list(range(0, 4)), list(range(4, 8)), list(range(8, NK))
+    b1 = blocks(ka, 5)
+    e1 = evac(ka, 5, b1)
+    b2 = blocks(kb, 6)
+    o1 = lists(ka, 2, 7, 0, e1)
+    e2 = evac(kb, 6, b2)
+    need("v", o1)
+    v_o1 = vcopy(T.offv[:, 0:128], ps[7][:, 0:128])
+    lists(kb, 2, 0, 0, e2)
+    o2 = lists(kb[3:], 0, 0, 128, e2)
+    b3 = blocks(kc, 1)
+
+    def gat(q, out, k, tok):
+        need(q, ("ldb", 16), tok)
+        src = T.tb_s[:, :].indirect(T.offv[:, 32 * k:32 * k + 32])
+        return vcopy(out, src) if q == "v" else act(out, src)
+
+    def sbc(k):
+        return T.sb[:, CAP * k:CAP * k + CAP]
+    tg = {}
+    tg[0] = gat("v", sbc(0), 0, v_o1)
+    tg[1] = gat("s", sbc(1), 1, v_o1)
+    tg[3] = gat("s", sbc(3), 3, v_o1)
+    need("v", o2)
+    vcopy(T.offv[:, 128:256], ps[0][:, 0:128])
+    v_o2 = vcopy(T.offu[:, 0:32], ps[0][:, 128:160])
+    tg[2] = gat("v", sbc(2), 2, v_o1)
+    e3 = evac(kc, 1, b3)
+    o3 = lists(kc, 0, 2, 0, e3)
+    tg[4] = gat("v", sbc(4), 4, v_o2)
+    tg[5] = gat("s", sbc(5), 5, v_o2)
+    tg[6] = gat("v", sbc(6), 6, v_o2)
+    tg[7] = gat("s", rcc(a), 7, v_o2)
+    need("v", o3)
+    v_o3 = vcopy(T.offu[:, 32:256], ps[2][:, 0:224])
+
+    sem_tb = T.sem["tb%d" % a]
+    for k, d in list(enumerate(off + near)):
+        need("g", tg[k])
+        if k >= len(off):
+            fused([(sbc(k), rcc(a), [d], me["min"], sem_tb)])
+        elif port:
+            fused([(sbc(k), rcc(a), [d], me["moff"], sem_tb)])
+        else:
+            h = me["bulk"][k % len(me["bulk"])]
+            q = rk[d]
+            fused([(sbc(k), rcc(q), [h], me["moff"], T.sem["tb%d" % q])])
+
+    need("v", k_jl, v_pf)
+    ts(T.m16[:, 0:128], T.jl[:], T.pf[:, 3:4], None, A.is_equal)
+    x = ts(T.ry[:, 0:128], T.jl[:], 0.0, None, A.not_equal)
+    n = 128
+    while n < 1024:
+        need("v", x)
+        vcopy(T.m16[:, n:2 * n], T.m16[:, 0:n])
+        x = vcopy(T.ry[:, n:2 * n], T.ry[:, 0:n])
+        n *= 2
+    v_z = did("v", V.memset(T.scw[:, 0:1], 0.0))
+
+    pbank = [3, 4, 5, 6]
+    t_mm, t_ev = {}, {}
+    for i, c in enumerate([core] + srcs):
+        r = rk[c]
+        if c == core:
+            need("v", tg[7], v_o2)
+        elif c in near:
+            need("v", ("tb%d" % r, count(P[c]["min"])), v_o3)
+        else:
+            need("v", ("tb%d" % r, count(P[c]["moff"] if P[c]["port"] else topo.mask(P[c]["bulk"][0], core))), v_o3)
+        need("v", ("lda", 16), t_mm.get(i - 4))
+        pr = T.pr[:, CAP * (i % 4):CAP * (i % 4) + CAP]
+        x = tt(pr, T.ta_s[:, :].indirect(T.offu[:, 32 * i:32 * i + 32]), rcc(r), A.mult)
+        need("p", x, t_ev.get(i - 4))
+        t_mm[i] = mm(ps[pbank[i % 4]][:], T.onef[:], pr, True, True)
+        need("s", t_mm[i])
+        t_ev[i] = act(T.scw[:, 1 + CAP * i:1 + CAP * i + CAP], ps[pbank[i % 4]][:])
+
+    need("v", t_ev[7], v_z, v_gp)
+    b0 = min(rk[d] for d in off)
+    n0 = min(rk[d] for d in near + [core])
+
+    def back(r0):
+        o = 256 * r0
+        x = tt(T.fin[:, o:o + 1024], T.scw[:, 0:4097].indirect(T.gpos[:, 16 * r0:16 * r0 + 64]), T.m16[:], A.mult)
+        need("v", x)
+        x = did("v", V.tensor_tensor_scan(T.fsc[:, o:o + 1024], T.ry[:], T.fin[:, o:o + 1024], 0.0, A.mult, A.add))
+        need("v", x)
+        return vcopy(T.yp[:, 16 * r0:16 * r0 + 64], T.fsc[:, o + 15:o + 1024:16])
+
+    def ypc(r):
+        return T.yp[:, 16 * r:16 * r + 16]
+    need("g", back(b0))
+    if port:
+        ms = split(me["moff"], len(off))
+        fused([(ypc(rk[d]), ylc(a), [d], ms[i], T.sem.ya) for i, d in enumerate(off)])
+    else:
+        fused([(T.yp[:, 16 * b0:16 * b0 + 64], T.yh[:], [me["small"]], me["mon"], T.sem.hy)])
+    x = back(n0)
+    need("g", x)
+    ms = split(me["mon"], len(near))
+    fused([(ypc(rk[d]), ylc(a), [d], ms[i], T.sem.ya) for i, d in enumerate(near)])
+    need("v", x)
+    x = vcopy(ylc(a), ypc(a))
+    n_y = 0
+    for c in cores:
+        if c == core:
+            continue
+        p = P[c]
+        if c in near:
+            n_y += count(split(p["mon"], len(p["near"]))[0])
+        else:
+            n_y += count(split(p["moff"] if p["port"] else topo.mask(p["small"], core), len(p["off"]))[0])
+    need("v", x, ("ya", n_y))
+    x = tt(T.y1[:], T.yl[:, 0:64], T.yl[:, 64:128], A.add)
+    need("v", x)
+    x = tt(T.y2[:], T.y1[:, 0:32], T.y1[:, 32:64], A.add)
+    need("v", x)
+    x = tt(T.y3[:], T.y2[:, 0:16], T.y2[:, 16:32], A.add)
+    need("y", x)
+    g.sync.dma_start(T.y[:], T.y3[:]).then_inc(T.sem.dy, 16)
+    need("y", ("dy", 16))
+    need("g", ("ls", ls["ls"]))
+    for q in done:
+        need("g", (psem[q], done[q]))

@@ -6,6 +6,9 @@ CAP = 512
 TRASH = 2048
 NK = 15
 SIM = 64
+PRE = 1024
+Z0 = 4
+ZS = NK * 128
 A = AluOpType
 COPY = ActivationFunctionType.Copy
 
@@ -28,15 +31,17 @@ SCRATCH = {
     "wt": ("sbuf", [128, 4], "bfloat16"), "di": ("sbuf", [128, 128], "float32"), "jl": ("sbuf", [128, 128], "float32"),
     "t16": ("sbuf", [128, 128], "float32"), "tr": ("sbuf", [128, 128], "float32"),
     "ident": ("sbuf", [128, 128], "bfloat16"), "nu": ("sbuf", [128, 128], "bfloat16"), "one": ("sbuf", [128, 128], "bfloat16"),
-    "onef": ("sbuf", [128, 128], "float32"), "bi": ("sbuf", [128, NK * 128], "bfloat16"), "lk": ("sbuf", [128, 8 * 128], "bfloat16"),
+    "idf": ("sbuf", [128, 128], "float32"), "onef": ("sbuf", [128, 128], "float32"),
+    "bi": ("sbuf", [128, NK * 128], "bfloat16"), "lk": ("sbuf", [128, 8 * 128], "bfloat16"),
     "m16": ("sbuf", [128, 1024], "bfloat16"), "ry": ("sbuf", [128, 1024], "bfloat16"),
-    "scw": ("sbuf", [128, 4100], "float32"), "fin": ("sbuf", [128, 2048], "float32"), "fsc": ("sbuf", [128, 2048], "float32"),
-    "yp": ("sbuf", [128, 128], "float32"), "yl": ("sbuf", [128, 128], "float32"), "yh": ("sbuf", [128, 64], "float32"),
-    "y1": ("sbuf", [128, 64], "float32"), "y2": ("sbuf", [128, 32], "float32"), "y3": ("sbuf", [128, 16], "float32"),
+    "scw": ("sbuf", [128, Z0 + NR * CAP], "float32"), "fin": ("sbuf", [128, 2048], "float32"), "fsc": ("sbuf", [128, 2048], "float32"),
+    "yp": ("sbuf", [128, 128], "float32"), "yl": ("sbuf", [128, 96], "float32"), "yh": ("sbuf", [128, 64], "float32"),
+    "ys": ("sbuf", [128, 64], "float32"), "yt": ("sbuf", [128, 80], "float32"),
 }
 for _i in range(8):
     SCRATCH["ps%d" % _i] = ("psum", [128, 512], "float32")
-SEMAPHORES = ["sv", "ss", "sp", "sg", "dn", "dw", "lda", "ldb", "dy", "ls0", "ls", "cla", "wla", "ya", "hy"] + ["tb%d" % _i for _i in range(NR)]
+SEMAPHORES = ["sv", "ss", "sp", "sg", "dn", "dw", "lda", "ldb", "dy", "ls0", "ls", "cla", "cp", "wln", "wla", "ya", "hy"]
+SEMAPHORES += ["tb%d" % _i for _i in range(NR)] + ["tc%d" % _i for _i in range(NR)]
 
 
 def bits(mask):
@@ -61,18 +66,25 @@ def plan(cores, topo):
         on = [x for x in cores if topo.chip(x) == topo.chip(c)]
         off = [x for x in cores if topo.chip(x) != topo.chip(c)]
         s = on.index(c)
-        off = [off[(s + k) % len(off)] for k in range(len(off))]
-        near = [on[(s + k) % len(on)] for k in range(1, len(on))]
         port = all(topo.may_write(c, d) for d in off)
+        rot = s + 1 if port else s
+        off = [off[(rot + k) % len(off)] for k in range(len(off))]
+        near = [on[(s + k) % len(on)] for k in range(1, len(on))]
         far = topo.chip(off[0])
-        small, bulk = None, []
+        relay, bulk = None, []
         if not port:
-            free = [x for x in range(SIM) if x not in cores and topo.die(x) == topo.die(c) and all(topo.may_write(x, d) for d in off) and topo.may_write(c, x)]
-            small = [x for x in free if topo.chip(x) == topo.chip(c)][0]
-            bulk = [x for x in free if topo.mates(topo.chip(x), far) and topo.same_plane(topo.chip(x), topo.chip(c))]
+            relay = [x for x in on if topo.die(x) == topo.die(c) and all(topo.may_write(x, d) for d in off)][0]
+            bulk = [x for x in range(SIM) if x not in cores and topo.die(x) == topo.die(c) and topo.mates(topo.chip(x), far)
+                    and topo.same_plane(topo.chip(x), topo.chip(c)) and topo.may_write(c, x) and all(topo.may_write(x, d) for d in off)]
         mon, moff = topo.mask(c, near[0]), topo.mask(c, off[0])
-        P[c] = {"near": near, "off": off, "port": port, "small": small, "bulk": bulk, "mon": mon, "moff": moff, "min": mon & ~moff}
+        P[c] = {"near": near, "off": off, "port": port, "relay": relay, "bulk": bulk, "mon": mon, "moff": moff, "min": mon & ~moff}
     return P
+
+
+def segments(P, c, d):
+    if d in P[c]["off"] and not P[c]["port"]:
+        return [(0, CAP // 2, "tb%d"), (CAP // 2, CAP, "tc%d")]
+    return [(0, CAP, "tb%d")]
 
 
 def rank_program(g, core, T, topo):
@@ -94,49 +106,39 @@ def rank_program(g, core, T, topo):
         g.remote_dma_fused([xfer(s, [d] * len(ids), ids, m, sem) for s, d, ids, m, sem in xs], local_sem=T.sem[lsem])
         ls[lsem] += sum(count(x[3]) for x in xs)
 
-    def clc(r):
-        return T.cl[:, 16 * r:16 * r + 16]
+    def clc(r, n=1):
+        return T.cl[:, 16 * r:16 * r + 16 * n]
 
     def wc(r):
         return T.w[:, 16 * r:16 * r + 16, :]
 
-    def rcc(r):
-        return T.rc[:, CAP * r:CAP * r + CAP]
+    def rcc(r, lo=0, hi=CAP):
+        return T.rc[:, CAP * r + lo:CAP * r + hi]
 
-    def ylc(r):
-        return T.yl[:, 16 * r:16 * r + 16]
+    def scc(i, lo=0, hi=CAP):
+        return T.scw[:, Z0 + CAP * i + lo:Z0 + CAP * i + hi]
 
     if rank is None:
         for c in cores:
             p = P[c]
             r = rk[c]
-            if p["port"]:
-                continue
-            if core == p["small"]:
-                mo = topo.mask(core, p["off"][0])
-                g.wait_ge(T.sem.cla, count(p["mon"]))
-                fused([(clc(r), clc(r), p["off"], mo, T.sem.cla)])
-                g.wait_ge(T.sem.hy, count(p["mon"]))
-                b0 = min(rk[d] for d in p["off"])
-                ms = split(mo, len(p["off"]))
-                fused([(T.yh[:, 16 * (rk[d] - b0):16 * (rk[d] - b0) + 16], ylc(r), [d], ms[i], T.sem.ya) for i, d in enumerate(p["off"])])
-                g.wait_ge(T.sem.ls, ls["ls"])
             if core in p["bulk"]:
-                nb = len(p["bulk"])
-                mine = p["off"][p["bulk"].index(core)::nb]
+                mine = p["off"][p["bulk"].index(core)::len(p["bulk"])]
                 mo = topo.mask(core, mine[0])
                 g.wait_ge(T.sem.wla, count(p["moff"]))
                 fused([(wc(r), wc(r), mine, mo, T.sem.wla)])
                 for d in mine:
                     q = rk[d]
-                    g.wait_ge(T.sem["tb%d" % q], count(p["moff"]))
-                    fused([(rcc(q), rcc(r), [d], mo, T.sem["tb%d" % r])])
+                    for lo, hi, sem in segments(P, c, d):
+                        g.wait_ge(T.sem[sem % q], count(p["moff"]))
+                        fused([(rcc(q, lo, hi), rcc(r, lo, hi), [d], mo, T.sem[sem % r])])
                 g.wait_ge(T.sem.ls, ls["ls"])
         return
 
     a = rank
     me = P[core]
     near, off, port = me["near"], me["off"], me["port"]
+    ward = [c for c in cores if P[c]["relay"] == core]
 
     eng = {"v": g.vector, "s": g.scalar, "p": g.tensor, "g": g, "y": g.sync}
     psem = {"v": "sv", "s": "ss", "p": "sp", "g": "sg"}
@@ -171,8 +173,8 @@ def rank_program(g, core, T, topo):
     def vcopy(out, x):
         return did("v", V.tensor_copy(out, x))
 
-    def act(out, x, **kw):
-        return did("s", S.activation(out, x, COPY, **kw))
+    def act(out, x, func=COPY, **kw):
+        return did("s", S.activation(out, x, func, **kw))
 
     def mm(out, l, r, st, sp):
         return did("p", PE.matmul(out, l, r, st, sp))
@@ -183,6 +185,7 @@ def rank_program(g, core, T, topo):
     g.sync.dma_start(T.wr[1::4, :], T.pi[:]).then_inc(T.sem.dw, 16)
     S.dma_start(T.wr[2::4, :], T.pj[:]).then_inc(T.sem.dw, 16)
     S.dma_start(T.wr[3::4, :], T.pj[:]).then_inc(T.sem.dw, 16)
+    g.sync.dma_start(T.tb_s[:, 0:PRE], T.tb[:, 0:PRE]).then_inc(T.sem.ldb, 16)
 
     F = dict(allow_small_or_imprecise_dtypes=True)
     k_pcol = did("g", g.iota(T.pcol[:], [[0, 1]], 0, 1))
@@ -191,16 +194,11 @@ def rank_program(g, core, T, topo):
     k_t16 = did("g", g.iota(T.t16[:], [[16, 128]], 0, 0, **F))
     k_jl = did("g", g.iota(T.jl[:], [[0, 8], [1, 16]], 0, 0, **F))
 
-    v_one = did("v", V.memset(T.one[:], 1.0))
-    did("v", V.memset(T.onef[:], 1.0))
-    v_r0 = did("v", V.memset(T.rst[:], 512.0))
     need("v", k_pcol)
     ts(T.pb[:, 0:1], T.pcol[:], 1, None, A.bitwise_and)
     ts(T.pb[:, 1:2], T.pcol[:], 3, None, A.bitwise_and)
     ts(T.pb[:, 2:3], T.pcol[:], 2, 3, A.arith_shift_right, A.bitwise_and)
     v_pb = ts(T.pb[:, 3:4], T.pcol[:], 15, None, A.bitwise_and)
-    need("v", v_r0)
-    v_rst = did("v", V.memset(T.rst[:, 0::128], -2.0))
     need("v", v_pb)
     v_pf = vcopy(T.pf[:], T.pb[:])
     need("v", k_di)
@@ -226,29 +224,50 @@ def rank_program(g, core, T, topo):
     need("v", x)
     for b in range(4):
         v_w = tt(T.w[:, 16 * a:16 * a + 16, b], T.wc[:, 16 * b:16 * b + 16], T.wd[:, 16 * b:16 * b + 16], A.add)
-    v_win = did("v", V.memset(T.win[:, TRASH:], 0.0))
+    v_one = did("v", V.memset(T.one[:], 1.0))
+    v_r0 = did("v", V.memset(T.rst[:], 512.0))
+    did("v", V.memset(T.onef[:], 1.0))
+    need("v", v_r0)
+    v_rst = did("v", V.memset(T.rst[:, 0::128], -2.0))
+    v_win = did("v", V.memset(T.win[:, TRASH + ZS:], 0.0))
+    need("v", k_jl, v_pf)
+    ts(T.m16[:, 0:128], T.jl[:], T.pf[:, 3:4], None, A.is_equal)
+    v_lane = ts(T.ry[:, 0:128], T.jl[:], 0.0, None, A.not_equal)
+    v_z = did("v", V.memset(T.scw[:, 0:Z0], 0.0))
+    v_idf = ts(T.idf[:], T.di[:], 0.0, None, A.is_equal)
 
+    few = split(me["min"], 2)[0]
+    t_cp = []
     need("g", v_cl)
     if port:
-        fused([(clc(a), clc(a), near, me["min"], T.sem.cla), (clc(a), clc(a), off, me["moff"], T.sem.cla)], "ls0")
+        fused([(clc(a), clc(a), near, me["moff"], T.sem.cla)], "ls0")
+        need("g", v_w)
+        fused([(wc(a), wc(a), near, me["min"], T.sem.wln)])
+        lo = min(a, rk[ward[0]])
+        t_cp = [("cp", count(P[ward[0]]["moff"]))]
+        need("g", t_cp)
+        fused([(clc(lo, 2), clc(lo, 2), off, me["moff"], T.sem.cla)], "ls0")
+        fused([(wc(a), wc(a), off, me["moff"], T.sem.wla)])
     else:
-        fused([(clc(a), clc(a), near + [me["small"]], me["mon"], T.sem.cla)], "ls0")
-    need("g", v_w)
-    fused([(wc(a), wc(a), near, me["min"], T.sem.wla), (wc(a), wc(a), off if port else me["bulk"], me["moff"], T.sem.wla)], "ls0")
-    n_cl, n_w = 0, 0
+        fused([(clc(a), clc(a), [c for c in near if c != me["relay"]], few, T.sem.cla),
+               (clc(a), clc(a), [me["relay"]], me["moff"], T.sem.cp)], "ls0")
+        need("g", v_w)
+        fused([(wc(a), wc(a), near, me["min"], T.sem.wln), (wc(a), wc(a), me["bulk"], me["moff"], T.sem.wla)])
+    n_cl, n_wn, n_w = 0, 0, 0
     for c in cores:
         p = P[c]
         if c == core:
             continue
         if c in near:
-            n_cl += count(p["min"] if p["port"] else p["mon"])
-            n_w += count(p["min"])
+            if c not in ward:
+                n_cl += count(p["moff"] if p["port"] else split(p["min"], 2)[0])
+            n_wn += count(p["min"])
         else:
-            n_cl += count(p["moff"] if p["port"] else topo.mask(p["small"], core))
+            n_cl += count(p["moff"]) if p["port"] else 0
             n_w += count(p["moff"] if p["port"] else topo.mask(p["bulk"][0], core))
 
     g.sync.wait_ge(T.sem.ls0, ls["ls0"])
-    g.sync.dma_start(T.tb_s[:], T.tb[:]).then_inc(T.sem.ldb, 16)
+    g.sync.dma_start(T.tb_s[:, PRE:], T.tb[:, PRE:]).then_inc(T.sem.ldb, 16)
     g.sync.dma_start(T.ta_s[:], T.ta[:]).then_inc(T.sem.lda, 16)
 
     need("g", v_one)
@@ -257,30 +276,54 @@ def rank_program(g, core, T, topo):
     need("s", v_id)
     for k in range(NK):
         s_bi = act(T.bi[:, 128 * k:128 * k + 128], T.ident[:], scale=float(TRASH + CAP * k + CAP // 2))
+    need("s", s_bi)
+    act(T.win[:, TRASH:TRASH + ZS], T.bi[:], scale=0.0)
+
+    n0 = min(rk[d] for d in near + [core])
+    b0 = min(rk[d] for d in off)
+
+    def places(r0, *toks):
+        need("s", *toks)
+        for yy in range(4):
+            for b in range(4):
+                o = 256 * r0 + 4 * yy + b
+                t = act(T.d[:, o:256 * r0 + 1024:16], T.w[:, 16 * r0:16 * r0 + 64, b], scale=T.my[:, yy:yy + 1])
+        return t
+    places(n0, ("wln", n_wn), v_w, v_my)
 
     def eta(c):
         if c in near:
-            return 2.0 + P[c]["near"].index(core)
-        return P[c]["off"].index(core) + (0.0 if P[c]["port"] else 1.2)
+            return 0.2 + 0.65 * P[c]["near"].index(core)
+        return P[c]["off"].index(core) + (0.0 if P[c]["port"] else 1.4)
     srcs = sorted([c for c in cores if c != core], key=eta)
-    cls = [8 * rk[d] + a for d in off + near] + [9 * a] + [8 * a + rk[c] for c in srcs]
+    dl = [off[0]] + [d for k in range(len(near)) for d in (near[k], off[k + 1])]
+    cls = [8 * rk[d] + a for d in dl] + [9 * a] + [8 * a + rk[c] for c in srcs]
     banks = [range(0, 4), range(4, 8), range(8, 12), range(12, NK)]
     ps = [T["ps%d" % i] for i in range(8)]
-    need("v", ("cla", n_cl), v_cl)
     tm, tsn = {}, {}
+
+    def kc_(buf, k):
+        return buf[:, 128 * k:128 * k + 128]
 
     def span(b):
         return slice(128 * banks[b][0], 128 * banks[b][-1] + 128)
+    need("v", ("cla", n_cl), t_cp, v_cl)
+    need("s", ("cla", n_cl), t_cp, v_cl)
+    for k in banks[3]:
+        x = act(kc_(T.z, k), T.cl[:], ActivationFunctionType.Abs, bias=-float(cls[k]))
+    need("s", x)
+    for k in banks[3]:
+        tm[3] = act(kc_(T.m, k), kc_(T.z, k), ActivationFunctionType.Relu, bias=1.0, scale=-1.0)
 
     def masks(b):
         for k in banks[b]:
-            tm[b] = ts(T.m[:, 128 * k:128 * k + 128], T.cl[:], float(cls[k]), None, A.is_equal)
+            tm[b] = ts(kc_(T.m, k), T.cl[:], float(cls[k]), None, A.is_equal)
 
     def scan(b):
         need("v", tm[b], v_rst)
         n = 128 * len(banks[b])
         tsn[b] = did("v", V.tensor_tensor_scan(T.s[:, span(b)], T.rst[:, 0:n], T.m[:, span(b)], -2.0, A.min, A.add))
-    masks(0); masks(1); scan(0); masks(2); scan(1); masks(3); scan(2); scan(3)
+    masks(0); masks(1); scan(0); masks(2); scan(1); scan(2); scan(3)
     first = [True]
 
     def p_nu(b):
@@ -290,7 +333,7 @@ def rank_program(g, core, T, topo):
     def p_base(b):
         need("p", tm[b], s_bi)
         for k in banks[b]:
-            mm(ps[4][:, 0:128], T.bi[:, 128 * k:128 * k + 128], T.m[:, 128 * k:128 * k + 128], first[0], False)
+            mm(ps[4][:, 0:128], kc_(T.bi, k), kc_(T.m, k), first[0], False)
             first[0] = False
     trank = {}
 
@@ -303,20 +346,24 @@ def rank_program(g, core, T, topo):
         x = tt(T.z[:, span(b)], ps[b][:, 0:128 * len(banks[b])], T.m[:, span(b)], A.mult)
         need("p", x, v_id)
         for k in banks[b]:
-            p_pos = mm(ps[4][:, 0:128], T.ident[:], T.z[:, 128 * k:128 * k + 128], False, k == NK - 1)
+            p_pos = mm(ps[4][:, 0:128], T.ident[:], kc_(T.z, k), False, k == NK - 1)
     need("v", p_pos, v_tr)
     v_posf = tt(T.posf[:], ps[4][:, 0:128], T.tr[:], A.max)
     need("v", v_posf)
     v_pos = vcopy(T.pos[:], T.posf[:])
 
-    need("s", ("wla", n_w), v_w, v_my)
-    for yy in range(4):
-        for b in range(4):
-            s_d = act(T.d[:, 4 * yy + b::16], T.w[:, :, b], scale=T.my[:, yy:yy + 1])
+    s_d = places(b0, ("wla", n_w))
+    n = 128
+    need("s", v_lane)
+    while n < 1024:
+        act(T.m16[:, n:2 * n], T.m16[:, 0:n])
+        s_lane = act(T.ry[:, n:2 * n], T.ry[:, 0:n])
+        need("s", s_lane)
+        n *= 2
 
     need("v", v_pos, s_d, v_win)
     v_sc = vcopy(T.win[:, :].indirect(T.pos[:, 0:128]), T.d[:])
-    v_gp = ts(T.gpos[:], T.posf[:], float(-(TRASH + 7 * CAP) + 1), 0.0, A.add, A.max)
+    v_gp = ts(T.gpos[:], T.posf[:], float(-(TRASH + 7 * CAP) + Z0), 0.0, A.add, A.max)
 
     def blocks(ks, bank):
         need("p", v_sc, v_wt)
@@ -336,92 +383,89 @@ def rank_program(g, core, T, topo):
         n = 4 * len(ks)
         for k in range(8):
             for q in range(2):
-                t = mm(ps[bank][:, o + k:o + 8 * n:8], T.lk[:, 128 * k:128 * k + 128], T.ev[:, 16 * ks[0] + qt + q:16 * ks[-1] + 16:4], q == 0, q == 1)
+                t = mm(ps[bank][:, o + k:o + 8 * n:8], kc_(T.lk, k), T.ev[:, 16 * ks[0] + qt + q:16 * ks[-1] + 16:4], q == 0, q == 1)
         return t
-    ka, kb, kc = list(range(0, 4)), list(range(4, 8)), list(range(8, NK))
+    ka, kb, kc = list(range(0, 2)), list(range(2, 8)), list(range(8, NK))
     b1 = blocks(ka, 5)
     e1 = evac(ka, 5, b1)
     b2 = blocks(kb, 6)
     o1 = lists(ka, 2, 7, 0, e1)
     e2 = evac(kb, 6, b2)
     need("v", o1)
-    v_o1 = vcopy(T.offv[:, 0:128], ps[7][:, 0:128])
+    v_o1 = vcopy(T.offv[:, 0:64], ps[7][:, 0:64])
     lists(kb, 2, 0, 0, e2)
-    o2 = lists(kb[3:], 0, 0, 128, e2)
+    o2 = lists(kb[5:], 0, 0, 192, e2)
     b3 = blocks(kc, 1)
 
-    def gat(q, out, k, tok):
-        need(q, ("ldb", 16), tok)
-        src = T.tb_s[:, :].indirect(T.offv[:, 32 * k:32 * k + 32])
-        return vcopy(out, src) if q == "v" else act(out, src)
+    H = CAP // 2
 
-    def sbc(k):
-        return T.sb[:, CAP * k:CAP * k + CAP]
+    def sbc(k, lo=0, hi=CAP):
+        return T.sb[:, CAP * k + lo:CAP * k + hi]
+
+    def gat(q, k, tok, lo=0, hi=CAP):
+        need(q, ("ldb", 32), tok)
+        src = T.tb_s[:, :].indirect(T.offv[:, 32 * k + lo // 16:32 * k + hi // 16])
+        out = rcc(a) if k == 7 else sbc(k, lo, hi)
+        return vcopy(out, src) if q == "v" else act(out, src)
     tg = {}
-    tg[0] = gat("v", sbc(0), 0, v_o1)
-    tg[1] = gat("s", sbc(1), 1, v_o1)
-    tg[3] = gat("s", sbc(3), 3, v_o1)
+    tg[0] = [gat("v", 0, v_o1, 0, H), gat("s", 0, v_o1, H, CAP)]
+    tg[1] = gat("s", 1, v_o1)
     need("v", o2)
-    vcopy(T.offv[:, 128:256], ps[0][:, 0:128])
-    v_o2 = vcopy(T.offu[:, 0:32], ps[0][:, 128:160])
-    tg[2] = gat("v", sbc(2), 2, v_o1)
+    vcopy(T.offv[:, 64:256], ps[0][:, 0:192])
+    v_o2 = vcopy(T.offu[:, 0:32], ps[0][:, 192:224])
+    for q, k in (("v", 2), ("s", 7), ("s", 3), ("s", 5)):
+        tg[k] = gat(q, k, v_o2)
     e3 = evac(kc, 1, b3)
     o3 = lists(kc, 0, 2, 0, e3)
-    tg[4] = gat("v", sbc(4), 4, v_o2)
-    tg[5] = gat("s", sbc(5), 5, v_o2)
-    tg[6] = gat("v", sbc(6), 6, v_o2)
-    tg[7] = gat("s", rcc(a), 7, v_o2)
+    for q, k in (("v", 4), ("s", 6)):
+        tg[k] = gat(q, k, v_o2)
     need("v", o3)
     v_o3 = vcopy(T.offu[:, 32:256], ps[2][:, 0:224])
 
-    sem_tb = T.sem["tb%d" % a]
-    for k, d in list(enumerate(off + near)):
-        need("g", tg[k])
-        if k >= len(off):
-            fused([(sbc(k), rcc(a), [d], me["min"], sem_tb)])
-        elif port:
-            fused([(sbc(k), rcc(a), [d], me["moff"], sem_tb)])
-        else:
-            h = me["bulk"][k % len(me["bulk"])]
-            q = rk[d]
-            fused([(sbc(k), rcc(q), [h], me["moff"], T.sem["tb%d" % q])])
-
-    need("v", k_jl, v_pf)
-    ts(T.m16[:, 0:128], T.jl[:], T.pf[:, 3:4], None, A.is_equal)
-    x = ts(T.ry[:, 0:128], T.jl[:], 0.0, None, A.not_equal)
-    n = 128
-    while n < 1024:
-        need("v", x)
-        vcopy(T.m16[:, n:2 * n], T.m16[:, 0:n])
-        x = vcopy(T.ry[:, n:2 * n], T.ry[:, 0:n])
-        n *= 2
-    v_z = did("v", V.memset(T.scw[:, 0:1], 0.0))
+    for k, d in enumerate(dl):
+        for lo, hi, sem in segments(P, core, d):
+            need("g", tg[k][0] if k == 0 and hi <= H else tg[k])
+            if d in near:
+                fused([(sbc(k, lo, hi), rcc(a, lo, hi), [d], me["min"], T.sem[sem % a])])
+            elif port:
+                fused([(sbc(k, lo, hi), rcc(a, lo, hi), [d], me["moff"], T.sem[sem % a])])
+            else:
+                h = me["bulk"][off.index(d) % len(me["bulk"])]
+                q = rk[d]
+                fused([(sbc(k, lo, hi), rcc(q, lo, hi), [h], me["moff"], T.sem[sem % q])])
 
     pbank = [3, 4, 5, 6]
     t_mm, t_ev = {}, {}
+    n = 0
     for i, c in enumerate([core] + srcs):
         r = rk[c]
-        if c == core:
-            need("v", tg[7], v_o2)
-        elif c in near:
-            need("v", ("tb%d" % r, count(P[c]["min"])), v_o3)
-        else:
-            need("v", ("tb%d" % r, count(P[c]["moff"] if P[c]["port"] else topo.mask(P[c]["bulk"][0], core))), v_o3)
-        need("v", ("lda", 16), t_mm.get(i - 4))
-        pr = T.pr[:, CAP * (i % 4):CAP * (i % 4) + CAP]
-        x = tt(pr, T.ta_s[:, :].indirect(T.offu[:, 32 * i:32 * i + 32]), rcc(r), A.mult)
-        need("p", x, t_ev.get(i - 4))
-        t_mm[i] = mm(ps[pbank[i % 4]][:], T.onef[:], pr, True, True)
-        need("s", t_mm[i])
-        t_ev[i] = act(T.scw[:, 1 + CAP * i:1 + CAP * i + CAP], ps[pbank[i % 4]][:])
+        for lo, hi, sem in ([(0, CAP, "")] if c == core else segments(P, c, core)):
+            if c == core:
+                need("v", tg[7], v_o2)
+            elif c in near:
+                need("v", (sem % r, count(P[c]["min"])), v_o3)
+            else:
+                need("v", (sem % r, count(P[c]["moff"] if P[c]["port"] else topo.mask(P[c]["bulk"][0], core))), v_o3)
+            need("v", ("lda", 16), t_mm.get(n - 4))
+            pr = T.pr[:, CAP * (n % 4):CAP * (n % 4) + hi - lo]
+            x = tt(pr, T.ta_s[:, :].indirect(T.offu[:, 32 * i + lo // 16:32 * i + hi // 16]), rcc(r, lo, hi), A.mult)
+            bank = ps[pbank[n % 4]][:, 0:hi - lo]
+            need("p", x, t_ev.get(n - 4))
+            t_mm[n] = mm(bank, T.onef[:], pr, True, True)
+            need("s", t_mm[n])
+            t_ev[n] = act(scc(i, lo, hi), bank)
+            n += 1
 
-    need("v", t_ev[7], v_z, v_gp)
-    b0 = min(rk[d] for d in off)
-    n0 = min(rk[d] for d in near + [core])
+    gives = {c: [x for x in cores if x == c or x in P[c]["near"]] + [x for x in P[c]["off"] if P[x]["port"]] for c in cores}
+
+    def yslot(d):
+        o = 16 * gives[d].index(core)
+        return T.yl[:, o:o + 16]
+    need("v", t_ev[n - 1], s_lane, v_z, v_gp)
 
     def back(r0):
         o = 256 * r0
-        x = tt(T.fin[:, o:o + 1024], T.scw[:, 0:4097].indirect(T.gpos[:, 16 * r0:16 * r0 + 64]), T.m16[:], A.mult)
+        x = tt(T.fin[:, o:o + 1024], T.scw[:, :].indirect(T.gpos[:, 16 * r0:16 * r0 + 64]), T.m16[:], A.mult)
         need("v", x)
         x = did("v", V.tensor_tensor_scan(T.fsc[:, o:o + 1024], T.ry[:], T.fin[:, o:o + 1024], 0.0, A.mult, A.add))
         need("v", x)
@@ -429,35 +473,39 @@ def rank_program(g, core, T, topo):
 
     def ypc(r):
         return T.yp[:, 16 * r:16 * r + 16]
-    need("g", back(b0))
+    xb = back(b0)
+    ms = split(me["moff"], len(off))
     if port:
-        ms = split(me["moff"], len(off))
-        fused([(ypc(rk[d]), ylc(a), [d], ms[i], T.sem.ya) for i, d in enumerate(off)])
+        need("p", xb, v_idf)
+        mm(ps[0][:, 0:64], T.idf[:], T.yp[:, 16 * b0:16 * b0 + 64], True, False)
+        need("p", ("hy", count(P[ward[0]]["mon"])))
+        need("s", mm(ps[0][:, 0:64], T.idf[:], T.yh[:], False, True))
+        need("g", act(T.ys[:], ps[0][:, 0:64]))
+        fused([(T.ys[:, 16 * (rk[d] - b0):16 * (rk[d] - b0) + 16], yslot(d), [d], ms[i], T.sem.ya) for i, d in enumerate(off)])
     else:
-        fused([(T.yp[:, 16 * b0:16 * b0 + 64], T.yh[:], [me["small"]], me["mon"], T.sem.hy)])
+        need("g", xb)
+        fused([(T.yp[:, 16 * b0:16 * b0 + 64], T.yh[:], [me["relay"]], me["mon"], T.sem.hy)])
     x = back(n0)
     need("g", x)
     ms = split(me["mon"], len(near))
-    fused([(ypc(rk[d]), ylc(a), [d], ms[i], T.sem.ya) for i, d in enumerate(near)])
+    fused([(ypc(rk[d]), yslot(d), [d], ms[i], T.sem.ya) for i, d in enumerate(near)])
     need("v", x)
-    x = vcopy(ylc(a), ypc(a))
+    x = vcopy(yslot(core), ypc(a))
     n_y = 0
-    for c in cores:
-        if c == core:
-            continue
+    for c in gives[core]:
         p = P[c]
         if c in near:
             n_y += count(split(p["mon"], len(p["near"]))[0])
-        else:
-            n_y += count(split(p["moff"] if p["port"] else topo.mask(p["small"], core), len(p["off"]))[0])
+        elif c != core:
+            n_y += count(split(p["moff"], len(p["off"]))[0])
     need("v", x, ("ya", n_y))
-    x = tt(T.y1[:], T.yl[:, 0:64], T.yl[:, 64:128], A.add)
+    x = tt(T.yt[:, 0:48], T.yl[:, 0:48], T.yl[:, 48:96], A.add)
     need("v", x)
-    x = tt(T.y2[:], T.y1[:, 0:32], T.y1[:, 32:64], A.add)
+    x = tt(T.yt[:, 48:64], T.yt[:, 0:16], T.yt[:, 16:32], A.add)
     need("v", x)
-    x = tt(T.y3[:], T.y2[:, 0:16], T.y2[:, 16:32], A.add)
+    x = tt(T.yt[:, 64:80], T.yt[:, 32:48], T.yt[:, 48:64], A.add)
     need("y", x)
-    g.sync.dma_start(T.y[:], T.y3[:]).then_inc(T.sem.dy, 16)
+    g.sync.dma_start(T.y[:], T.yt[:, 64:80]).then_inc(T.sem.dy, 16)
     need("y", ("dy", 16))
     need("g", ("ls", ls["ls"]))
     for q in done:

from concourse.bass import DstId, RemoteDMATransfer
from concourse.mybir import dt, AluOpType, AxisListType, ActivationFunctionType

NR = 8
CAP = 512
TRASH = 2048
NK = 15
SIM = 64
PRE = 1024
Z0 = 4
ZS = NK * 128
A = AluOpType
COPY = ActivationFunctionType.Copy

SCRATCH = {
    "ta_s": ("sbuf", [128, 4096], "float32"), "tb_s": ("sbuf", [128, 4096], "float32"),
    "sb": ("sbuf", [128, 7 * CAP], "float32"), "rc": ("sbuf", [128, NR * CAP], "float32"),
    "pr": ("sbuf", [128, 4 * CAP], "float32"),
    "ni": ("sbuf", [128, 16], "int32"), "nj": ("sbuf", [128, 16], "int32"), "wr": ("sbuf", [128, 64], "int32"),
    "t1": ("sbuf", [128, 16], "int32"), "t2": ("sbuf", [128, 16], "int32"),
    "wa": ("sbuf", [128, 64], "int32"), "wb": ("sbuf", [128, 64], "int32"),
    "wc": ("sbuf", [128, 64], "bfloat16"), "wd": ("sbuf", [128, 64], "bfloat16"),
    "cl": ("sbuf", [128, 128], "bfloat16"), "w": ("sbuf", [128, 128, 4], "bfloat16"),
    "d": ("sbuf", [128, 2048], "bfloat16"), "win": ("sbuf", [128, TRASH + NK * CAP], "bfloat16"),
    "m": ("sbuf", [128, NK * 128], "bfloat16"), "s": ("sbuf", [128, NK * 128], "bfloat16"),
    "z": ("sbuf", [128, NK * 128], "bfloat16"), "rst": ("sbuf", [128, 512], "bfloat16"),
    "posf": ("sbuf", [128, 128], "float32"), "pos": ("sbuf", [128, 128], "uint16"), "gpos": ("sbuf", [128, 128], "uint16"),
    "ev": ("sbuf", [128, NK * 16], "bfloat16"), "offv": ("sbuf", [128, 256], "uint16"), "offu": ("sbuf", [128, 256], "uint16"),
    "pcol": ("sbuf", [128, 1], "int32"), "pb": ("sbuf", [128, 4], "int32"), "pf": ("sbuf", [128, 4], "float32"),
    "mh": ("sbuf", [128, 1], "float32"), "q4": ("sbuf", [128, 4], "float32"), "my": ("sbuf", [128, 4], "float32"),
    "wt": ("sbuf", [128, 4], "bfloat16"), "di": ("sbuf", [128, 128], "float32"), "jl": ("sbuf", [128, 128], "float32"),
    "t16": ("sbuf", [128, 128], "float32"), "tr": ("sbuf", [128, 128], "float32"),
    "ident": ("sbuf", [128, 128], "bfloat16"), "nu": ("sbuf", [128, 128], "bfloat16"), "one": ("sbuf", [128, 128], "bfloat16"),
    "idf": ("sbuf", [128, 128], "float32"), "onef": ("sbuf", [128, 128], "float32"),
    "bi": ("sbuf", [128, NK * 128], "bfloat16"), "lk": ("sbuf", [128, 8 * 128], "bfloat16"),
    "m16": ("sbuf", [128, 1024], "bfloat16"), "ry": ("sbuf", [128, 1024], "bfloat16"),
    "scw": ("sbuf", [128, Z0 + NR * CAP], "float32"), "fin": ("sbuf", [128, 2048], "float32"), "fsc": ("sbuf", [128, 2048], "float32"),
    "yp": ("sbuf", [128, 128], "float32"), "yl": ("sbuf", [128, 96], "float32"), "yh": ("sbuf", [128, 64], "float32"),
    "ys": ("sbuf", [128, 64], "float32"), "yt": ("sbuf", [128, 80], "float32"),
}
for _i in range(8):
    SCRATCH["ps%d" % _i] = ("psum", [128, 512], "float32")
SEMAPHORES = ["sv", "ss", "sp", "sg", "dn", "dw", "lda", "ldb", "dy", "ls0", "ls", "cla", "cp", "wln", "wla", "ya", "hy"]
SEMAPHORES += ["tb%d" % _i for _i in range(NR)] + ["tc%d" % _i for _i in range(NR)]


def bits(mask):
    return [1 << e for e in range(32) if mask >> e & 1]


def split(mask, n):
    b = bits(mask)
    k = 1
    while 2 * k * n <= len(b):
        k *= 2
    return [sum(b[i * k:(i + 1) * k]) for i in range(n)]


def count(mask):
    return len(bits(mask))


def plan(cores, topo):
    P = {}
    for c in cores:
        on = [x for x in cores if topo.chip(x) == topo.chip(c)]
        off = [x for x in cores if topo.chip(x) != topo.chip(c)]
        s = on.index(c)
        port = all(topo.may_write(c, d) for d in off)
        rot = s + 1 if port else s
        off = [off[(rot + k) % len(off)] for k in range(len(off))]
        near = [on[(s + k) % len(on)] for k in range(1, len(on))]
        far = topo.chip(off[0])
        relay, bulk = None, []
        if not port:
            relay = [x for x in on if topo.die(x) == topo.die(c) and all(topo.may_write(x, d) for d in off)][0]
            bulk = [x for x in range(SIM) if x not in cores and topo.die(x) == topo.die(c) and topo.mates(topo.chip(x), far)
                    and topo.same_plane(topo.chip(x), topo.chip(c)) and topo.may_write(c, x) and all(topo.may_write(x, d) for d in off)]
        mon, moff = topo.mask(c, near[0]), topo.mask(c, off[0])
        P[c] = {"near": near, "off": off, "port": port, "relay": relay, "bulk": bulk, "mon": mon, "moff": moff, "min": mon & ~moff}
    return P


def segments(P, c, d):
    if d in P[c]["off"] and not P[c]["port"]:
        return [(0, CAP // 2, "tb%d"), (CAP // 2, CAP, "tc%d")]
    return [(0, CAP, "tb%d")]


def rank_program(g, core, T, topo):
    cores = list(T.cores)
    P = plan(cores, topo)
    rank = T.rank_of(core)
    rk = {c: i for i, c in enumerate(cores)}

    def dst(c):
        a = topo.addr(c)
        return DstId(rid=a[0], pnc=a[1])

    def xfer(src, dsts, ids, mask, sem):
        return RemoteDMATransfer(dst_ids=[dst(c) for c in ids], dma_engine_mask=mask, remote_sem=sem, srcs=[src], dsts=dsts)

    ls = {"ls0": 0, "ls": 0}

    def fused(xs, lsem="ls"):
        g.remote_dma_fused([xfer(s, [d] * len(ids), ids, m, sem) for s, d, ids, m, sem in xs], local_sem=T.sem[lsem])
        ls[lsem] += sum(count(x[3]) for x in xs)

    def clc(r, n=1):
        return T.cl[:, 16 * r:16 * r + 16 * n]

    def wc(r):
        return T.w[:, 16 * r:16 * r + 16, :]

    def rcc(r, lo=0, hi=CAP):
        return T.rc[:, CAP * r + lo:CAP * r + hi]

    def scc(i, lo=0, hi=CAP):
        return T.scw[:, Z0 + CAP * i + lo:Z0 + CAP * i + hi]

    if rank is None:
        for c in cores:
            p = P[c]
            r = rk[c]
            if core in p["bulk"]:
                mine = p["off"][p["bulk"].index(core)::len(p["bulk"])]
                mo = topo.mask(core, mine[0])
                g.wait_ge(T.sem.wla, count(p["moff"]))
                fused([(wc(r), wc(r), mine, mo, T.sem.wla)])
                for d in mine:
                    q = rk[d]
                    for lo, hi, sem in segments(P, c, d):
                        g.wait_ge(T.sem[sem % q], count(p["moff"]))
                        fused([(rcc(q, lo, hi), rcc(r, lo, hi), [d], mo, T.sem[sem % r])])
                g.wait_ge(T.sem.ls, ls["ls"])
        return

    a = rank
    me = P[core]
    near, off, port = me["near"], me["off"], me["port"]
    ward = [c for c in cores if P[c]["relay"] == core]

    eng = {"v": g.vector, "s": g.scalar, "p": g.tensor, "g": g, "y": g.sync}
    psem = {"v": "sv", "s": "ss", "p": "sp", "g": "sg"}
    done = {"v": 0, "s": 0, "p": 0, "g": 0}
    seen = {}

    def need(q, *toks):
        for t in toks:
            if t is None:
                continue
            if isinstance(t, list):
                need(q, *t)
                continue
            sem, val = t
            if seen.get((q, sem), 0) < val:
                eng[q].wait_ge(T.sem[sem], val)
                seen[(q, sem)] = val

    def did(q, ins):
        done[q] += 1
        ins.then_inc(T.sem[psem[q]], 1)
        return (psem[q], done[q])

    V, S, PE = g.vector, g.scalar, g.tensor

    def ts(out, in0, s1, s2, *ops):
        return did("v", V.tensor_scalar(out, in0, s1, s2, *ops))

    def tt(out, x, y, op):
        return did("v", V.tensor_tensor(out, x, y, op))

    def vcopy(out, x):
        return did("v", V.tensor_copy(out, x))

    def act(out, x, func=COPY, **kw):
        return did("s", S.activation(out, x, func, **kw))

    def mm(out, l, r, st, sp):
        return did("p", PE.matmul(out, l, r, st, sp))

    g.sync.dma_start(T.ni[:], T.pi[:]).then_inc(T.sem.dn, 16)
    S.dma_start(T.nj[:], T.pj[:]).then_inc(T.sem.dn, 16)
    g.sync.dma_start(T.wr[0::4, :], T.pi[:]).then_inc(T.sem.dw, 16)
    g.sync.dma_start(T.wr[1::4, :], T.pi[:]).then_inc(T.sem.dw, 16)
    S.dma_start(T.wr[2::4, :], T.pj[:]).then_inc(T.sem.dw, 16)
    S.dma_start(T.wr[3::4, :], T.pj[:]).then_inc(T.sem.dw, 16)
    g.sync.dma_start(T.tb_s[:, 0:PRE], T.tb[:, 0:PRE]).then_inc(T.sem.ldb, 16)

    F = dict(allow_small_or_imprecise_dtypes=True)
    k_pcol = did("g", g.iota(T.pcol[:], [[0, 1]], 0, 1))
    k_di = did("g", g.iota(T.di[:], [[1, 128]], 0, -1, **F))
    k_q4 = did("g", g.iota(T.q4[:], [[1, 4]], 0, 0, **F))
    k_t16 = did("g", g.iota(T.t16[:], [[16, 128]], 0, 0, **F))
    k_jl = did("g", g.iota(T.jl[:], [[0, 8], [1, 16]], 0, 0, **F))

    need("v", k_pcol)
    ts(T.pb[:, 0:1], T.pcol[:], 1, None, A.bitwise_and)
    ts(T.pb[:, 1:2], T.pcol[:], 3, None, A.bitwise_and)
    ts(T.pb[:, 2:3], T.pcol[:], 2, 3, A.arith_shift_right, A.bitwise_and)
    v_pb = ts(T.pb[:, 3:4], T.pcol[:], 15, None, A.bitwise_and)
    need("v", v_pb)
    v_pf = vcopy(T.pf[:], T.pb[:])
    need("v", k_di)
    v_id = ts(T.ident[:], T.di[:], 0.0, None, A.is_equal)
    v_nu = ts(T.nu[:], T.di[:], 0.0, -1.0, A.is_le, A.mult)
    need("v", v_pf, k_q4, k_t16)
    v_mh = ts(T.mh[:], T.pf[:, 0:1], 0.0, None, A.is_equal)
    v_wt = ts(T.wt[:], T.q4[:], T.pf[:, 1:2], None, A.is_equal)
    v_my = ts(T.my[:], T.q4[:], T.pf[:, 2:3], None, A.is_equal)
    v_tr = ts(T.tr[:], T.t16[:], T.pf[:, 3:4], None, A.add)

    need("v", ("dn", 32))
    ts(T.t1[:], T.ni[:], 9, 56, A.arith_shift_right, A.bitwise_and)
    x = ts(T.t2[:], T.nj[:], 12, None, A.arith_shift_right)
    need("v", x)
    v_cl = tt(clc(a), T.t1[:], T.t2[:], A.add)
    need("v", ("dw", 64))
    ts(T.wa[:], T.wr[:], 4032, None, A.bitwise_and)
    x = ts(T.wb[:], T.wr[:], 63, None, A.bitwise_and)
    need("v", x, v_mh)
    ts(T.wc[:], T.wa[:], T.mh[:, 0:1], None, A.mult)
    x = ts(T.wd[:], T.wb[:], T.pf[:, 0:1], None, A.mult)
    need("v", x)
    for b in range(4):
        v_w = tt(T.w[:, 16 * a:16 * a + 16, b], T.wc[:, 16 * b:16 * b + 16], T.wd[:, 16 * b:16 * b + 16], A.add)
    v_one = did("v", V.memset(T.one[:], 1.0))
    v_r0 = did("v", V.memset(T.rst[:], 512.0))
    did("v", V.memset(T.onef[:], 1.0))
    need("v", v_r0)
    v_rst = did("v", V.memset(T.rst[:, 0::128], -2.0))
    v_win = did("v", V.memset(T.win[:, TRASH + ZS:], 0.0))
    need("v", k_jl, v_pf)
    ts(T.m16[:, 0:128], T.jl[:], T.pf[:, 3:4], None, A.is_equal)
    v_lane = ts(T.ry[:, 0:128], T.jl[:], 0.0, None, A.not_equal)
    v_z = did("v", V.memset(T.scw[:, 0:Z0], 0.0))
    v_idf = ts(T.idf[:], T.di[:], 0.0, None, A.is_equal)

    few = split(me["min"], 2)[0]
    t_cp = []
    need("g", v_cl)
    if port:
        fused([(clc(a), clc(a), near, me["moff"], T.sem.cla)], "ls0")
        need("g", v_w)
        fused([(wc(a), wc(a), near, me["min"], T.sem.wln)])
        lo = min(a, rk[ward[0]])
        t_cp = [("cp", count(P[ward[0]]["moff"]))]
        need("g", t_cp)
        fused([(clc(lo, 2), clc(lo, 2), off, me["moff"], T.sem.cla)], "ls0")
        fused([(wc(a), wc(a), off, me["moff"], T.sem.wla)])
    else:
        fused([(clc(a), clc(a), [c for c in near if c != me["relay"]], few, T.sem.cla),
               (clc(a), clc(a), [me["relay"]], me["moff"], T.sem.cp)], "ls0")
        need("g", v_w)
        fused([(wc(a), wc(a), near, me["min"], T.sem.wln), (wc(a), wc(a), me["bulk"], me["moff"], T.sem.wla)])
    n_cl, n_wn, n_w = 0, 0, 0
    for c in cores:
        p = P[c]
        if c == core:
            continue
        if c in near:
            if c not in ward:
                n_cl += count(p["moff"] if p["port"] else split(p["min"], 2)[0])
            n_wn += count(p["min"])
        else:
            n_cl += count(p["moff"]) if p["port"] else 0
            n_w += count(p["moff"] if p["port"] else topo.mask(p["bulk"][0], core))

    g.sync.wait_ge(T.sem.ls0, ls["ls0"])
    g.sync.dma_start(T.tb_s[:, PRE:], T.tb[:, PRE:]).then_inc(T.sem.ldb, 16)
    g.sync.dma_start(T.ta_s[:], T.ta[:]).then_inc(T.sem.lda, 16)

    need("g", v_one)
    for k in range(8):
        g_lk = did("g", g.affine_select(T.lk[:, 128 * k:128 * k + 128], T.one[:], [[0, 8], [-1, 16]], A.is_equal, 0.0, -16 * k, 1))
    need("s", v_id)
    for k in range(NK):
        s_bi = act(T.bi[:, 128 * k:128 * k + 128], T.ident[:], scale=float(TRASH + CAP * k + CAP // 2))
    need("s", s_bi)
    act(T.win[:, TRASH:TRASH + ZS], T.bi[:], scale=0.0)

    n0 = min(rk[d] for d in near + [core])
    b0 = min(rk[d] for d in off)

    def places(r0, *toks):
        need("s", *toks)
        for yy in range(4):
            for b in range(4):
                o = 256 * r0 + 4 * yy + b
                t = act(T.d[:, o:256 * r0 + 1024:16], T.w[:, 16 * r0:16 * r0 + 64, b], scale=T.my[:, yy:yy + 1])
        return t
    places(n0, ("wln", n_wn), v_w, v_my)

    def eta(c):
        if c in near:
            return 0.2 + 0.65 * P[c]["near"].index(core)
        return P[c]["off"].index(core) + (0.0 if P[c]["port"] else 1.4)
    srcs = sorted([c for c in cores if c != core], key=eta)
    dl = [off[0]] + [d for k in range(len(near)) for d in (near[k], off[k + 1])]
    cls = [8 * rk[d] + a for d in dl] + [9 * a] + [8 * a + rk[c] for c in srcs]
    banks = [range(0, 4), range(4, 8), range(8, 12), range(12, NK)]
    ps = [T["ps%d" % i] for i in range(8)]
    tm, tsn = {}, {}

    def kc_(buf, k):
        return buf[:, 128 * k:128 * k + 128]

    def span(b):
        return slice(128 * banks[b][0], 128 * banks[b][-1] + 128)
    need("v", ("cla", n_cl), t_cp, v_cl)
    need("s", ("cla", n_cl), t_cp, v_cl)
    for k in banks[3]:
        x = act(kc_(T.z, k), T.cl[:], ActivationFunctionType.Abs, bias=-float(cls[k]))
    need("s", x)
    for k in banks[3]:
        tm[3] = act(kc_(T.m, k), kc_(T.z, k), ActivationFunctionType.Relu, bias=1.0, scale=-1.0)

    def masks(b):
        for k in banks[b]:
            tm[b] = ts(kc_(T.m, k), T.cl[:], float(cls[k]), None, A.is_equal)

    def scan(b):
        need("v", tm[b], v_rst)
        n = 128 * len(banks[b])
        tsn[b] = did("v", V.tensor_tensor_scan(T.s[:, span(b)], T.rst[:, 0:n], T.m[:, span(b)], -2.0, A.min, A.add))
    masks(0); masks(1); scan(0); masks(2); scan(1); scan(2); scan(3)
    first = [True]

    def p_nu(b):
        need("p", tm[b], v_nu, v_one)
        mm(ps[b][:, 0:128 * len(banks[b])], T.nu[:], T.m[:, span(b)], True, False)

    def p_base(b):
        need("p", tm[b], s_bi)
        for k in banks[b]:
            mm(ps[4][:, 0:128], kc_(T.bi, k), kc_(T.m, k), first[0], False)
            first[0] = False
    trank = {}

    def p_s(b):
        need("p", tsn[b])
        trank[b] = mm(ps[b][:, 0:128 * len(banks[b])], T.one[:], T.s[:, span(b)], False, True)
    p_nu(0); p_base(0); p_nu(1); p_s(0); p_base(1); p_nu(2); p_s(1); p_base(2); p_nu(3); p_s(2); p_s(3); p_base(3)
    for b in range(4):
        need("v", trank[b])
        x = tt(T.z[:, span(b)], ps[b][:, 0:128 * len(banks[b])], T.m[:, span(b)], A.mult)
        need("p", x, v_id)
        for k in banks[b]:
            p_pos = mm(ps[4][:, 0:128], T.ident[:], kc_(T.z, k), False, k == NK - 1)
    need("v", p_pos, v_tr)
    v_posf = tt(T.posf[:], ps[4][:, 0:128], T.tr[:], A.max)
    need("v", v_posf)
    v_pos = vcopy(T.pos[:], T.posf[:])

    s_d = places(b0, ("wla", n_w))
    n = 128
    need("s", v_lane)
    while n < 1024:
        act(T.m16[:, n:2 * n], T.m16[:, 0:n])
        s_lane = act(T.ry[:, n:2 * n], T.ry[:, 0:n])
        need("s", s_lane)
        n *= 2

    need("v", v_pos, s_d, v_win)
    v_sc = vcopy(T.win[:, :].indirect(T.pos[:, 0:128]), T.d[:])
    v_gp = ts(T.gpos[:], T.posf[:], float(-(TRASH + 7 * CAP) + Z0), 0.0, A.add, A.max)

    def blocks(ks, bank):
        need("p", v_sc, v_wt)
        for k in ks:
            for j in range(4):
                c0 = TRASH + CAP * k + 128 * j
                o = 4 * (4 * (k - ks[0]) + j)
                t = mm(ps[bank][:, o:o + 4], T.win[:, c0:c0 + 128], T.wt[:], True, True)
        return t

    def evac(ks, bank, tok):
        need("v", tok)
        return vcopy(T.ev[:, 16 * ks[0]:16 * ks[-1] + 16], ps[bank][:, 0:16 * len(ks)])

    def lists(ks, qt, bank, o, tok):
        need("p", tok, g_lk)
        n = 4 * len(ks)
        for k in range(8):
            for q in range(2):
                t = mm(ps[bank][:, o + k:o + 8 * n:8], kc_(T.lk, k), T.ev[:, 16 * ks[0] + qt + q:16 * ks[-1] + 16:4], q == 0, q == 1)
        return t
    ka, kb, kc = list(range(0, 2)), list(range(2, 8)), list(range(8, NK))
    b1 = blocks(ka, 5)
    e1 = evac(ka, 5, b1)
    b2 = blocks(kb, 6)
    o1 = lists(ka, 2, 7, 0, e1)
    e2 = evac(kb, 6, b2)
    need("v", o1)
    v_o1 = vcopy(T.offv[:, 0:64], ps[7][:, 0:64])
    lists(kb, 2, 0, 0, e2)
    o2 = lists(kb[5:], 0, 0, 192, e2)
    b3 = blocks(kc, 1)

    H = CAP // 2

    def sbc(k, lo=0, hi=CAP):
        return T.sb[:, CAP * k + lo:CAP * k + hi]

    def gat(q, k, tok, lo=0, hi=CAP):
        need(q, ("ldb", 32), tok)
        src = T.tb_s[:, :].indirect(T.offv[:, 32 * k + lo // 16:32 * k + hi // 16])
        out = rcc(a) if k == 7 else sbc(k, lo, hi)
        return vcopy(out, src) if q == "v" else act(out, src)
    tg = {}
    tg[0] = [gat("v", 0, v_o1, 0, H), gat("s", 0, v_o1, H, CAP)]
    tg[1] = gat("s", 1, v_o1)
    need("v", o2)
    vcopy(T.offv[:, 64:256], ps[0][:, 0:192])
    v_o2 = vcopy(T.offu[:, 0:32], ps[0][:, 192:224])
    for q, k in (("v", 2), ("s", 7), ("s", 3), ("s", 5)):
        tg[k] = gat(q, k, v_o2)
    e3 = evac(kc, 1, b3)
    o3 = lists(kc, 0, 2, 0, e3)
    for q, k in (("v", 4), ("s", 6)):
        tg[k] = gat(q, k, v_o2)
    need("v", o3)
    v_o3 = vcopy(T.offu[:, 32:256], ps[2][:, 0:224])

    for k, d in enumerate(dl):
        for lo, hi, sem in segments(P, core, d):
            need("g", tg[k][0] if k == 0 and hi <= H else tg[k])
            if d in near:
                fused([(sbc(k, lo, hi), rcc(a, lo, hi), [d], me["min"], T.sem[sem % a])])
            elif port:
                fused([(sbc(k, lo, hi), rcc(a, lo, hi), [d], me["moff"], T.sem[sem % a])])
            else:
                h = me["bulk"][off.index(d) % len(me["bulk"])]
                q = rk[d]
                fused([(sbc(k, lo, hi), rcc(q, lo, hi), [h], me["moff"], T.sem[sem % q])])

    pbank = [3, 4, 5, 6]
    t_mm, t_ev = {}, {}
    n = 0
    for i, c in enumerate([core] + srcs):
        r = rk[c]
        for lo, hi, sem in ([(0, CAP, "")] if c == core else segments(P, c, core)):
            if c == core:
                need("v", tg[7], v_o2)
            elif c in near:
                need("v", (sem % r, count(P[c]["min"])), v_o3)
            else:
                need("v", (sem % r, count(P[c]["moff"] if P[c]["port"] else topo.mask(P[c]["bulk"][0], core))), v_o3)
            need("v", ("lda", 16), t_mm.get(n - 4))
            pr = T.pr[:, CAP * (n % 4):CAP * (n % 4) + hi - lo]
            x = tt(pr, T.ta_s[:, :].indirect(T.offu[:, 32 * i + lo // 16:32 * i + hi // 16]), rcc(r, lo, hi), A.mult)
            bank = ps[pbank[n % 4]][:, 0:hi - lo]
            need("p", x, t_ev.get(n - 4))
            t_mm[n] = mm(bank, T.onef[:], pr, True, True)
            need("s", t_mm[n])
            t_ev[n] = act(scc(i, lo, hi), bank)
            n += 1

    gives = {c: [x for x in cores if x == c or x in P[c]["near"]] + [x for x in P[c]["off"] if P[x]["port"]] for c in cores}

    def yslot(d):
        o = 16 * gives[d].index(core)
        return T.yl[:, o:o + 16]
    need("v", t_ev[n - 1], s_lane, v_z, v_gp)

    def back(r0):
        o = 256 * r0
        x = tt(T.fin[:, o:o + 1024], T.scw[:, :].indirect(T.gpos[:, 16 * r0:16 * r0 + 64]), T.m16[:], A.mult)
        need("v", x)
        x = did("v", V.tensor_tensor_scan(T.fsc[:, o:o + 1024], T.ry[:], T.fin[:, o:o + 1024], 0.0, A.mult, A.add))
        need("v", x)
        return vcopy(T.yp[:, 16 * r0:16 * r0 + 64], T.fsc[:, o + 15:o + 1024:16])

    def ypc(r):
        return T.yp[:, 16 * r:16 * r + 16]
    xb = back(b0)
    ms = split(me["moff"], len(off))
    if port:
        need("p", xb, v_idf)
        mm(ps[0][:, 0:64], T.idf[:], T.yp[:, 16 * b0:16 * b0 + 64], True, False)
        need("p", ("hy", count(P[ward[0]]["mon"])))
        need("s", mm(ps[0][:, 0:64], T.idf[:], T.yh[:], False, True))
        need("g", act(T.ys[:], ps[0][:, 0:64]))
        fused([(T.ys[:, 16 * (rk[d] - b0):16 * (rk[d] - b0) + 16], yslot(d), [d], ms[i], T.sem.ya) for i, d in enumerate(off)])
    else:
        need("g", xb)
        fused([(T.yp[:, 16 * b0:16 * b0 + 64], T.yh[:], [me["relay"]], me["mon"], T.sem.hy)])
    x = back(n0)
    need("g", x)
    ms = split(me["mon"], len(near))
    fused([(ypc(rk[d]), yslot(d), [d], ms[i], T.sem.ya) for i, d in enumerate(near)])
    need("v", x)
    x = vcopy(yslot(core), ypc(a))
    n_y = 0
    for c in gives[core]:
        p = P[c]
        if c in near:
            n_y += count(split(p["mon"], len(p["near"]))[0])
        elif c != core:
            n_y += count(split(p["moff"], len(p["off"]))[0])
    need("v", x, ("ya", n_y))
    x = tt(T.yt[:, 0:48], T.yl[:, 0:48], T.yl[:, 48:96], A.add)
    need("v", x)
    x = tt(T.yt[:, 48:64], T.yt[:, 0:16], T.yt[:, 16:32], A.add)
    need("v", x)
    x = tt(T.yt[:, 64:80], T.yt[:, 32:48], T.yt[:, 48:64], A.add)
    need("y", x)
    g.sync.dma_start(T.y[:], T.yt[:, 64:80]).then_inc(T.sem.dy, 16)
    need("y", ("dy", 16))
    need("g", ("ls", ls["ls"]))
    for q in done:
        need("g", (psem[q], done[q]))
